import numpy as np
import ml_dtypes


def mxq(x, axis, fmt="e4m3"):
    dtype, down = {"e4m3": (ml_dtypes.float8_e4m3fn, 7), "e5m2": (ml_dtypes.float8_e5m2, 14)}[fmt]
    v = np.moveaxis(np.asarray(x, np.float32).astype(ml_dtypes.bfloat16).astype(np.float64), axis, -1)
    blocks = v.reshape(v.shape[:-1] + (-1, 32))
    amax = np.abs(blocks).max(-1, keepdims=True)
    byte = np.maximum(np.where(amax > 0, np.frexp(amax)[1] - 1 + 127, 0) - down, 1)
    scale = np.exp2(byte - 127.0)
    codes = (blocks / scale).astype(np.float32).astype(dtype).astype(np.float64)
    return np.moveaxis((codes * scale).reshape(v.shape), -1, axis)


WIDE = False


def mx_kscale(k):
    if not WIDE:
        return np.ones(k)
    levels = np.array([10, -10, 5, -5, 0])
    if k % 512:
        return np.exp2(np.random.permutation(np.resize(levels, k // 32))).repeat(32)
    a = np.empty((k // 512, 16))
    for p in range(k // 512):
        a[p, :8] = np.random.permutation(np.resize(levels, 8))
        for g in range(8):
            far = levels[np.abs(levels - a[p, g]) >= 10]
            a[p, g + 8] = far[np.random.randint(len(far))]
    return np.exp2(a.ravel()).repeat(32)


def f64(x):
    return np.asarray(x).astype(np.float64)


def striped8(idx):
    return np.asarray(idx).reshape(8, -1, 16).transpose(0, 2, 1).reshape(128, -1).astype(np.uint16)


def unstriped8(offs):
    return offs.reshape(8, 16, -1).transpose(0, 2, 1).reshape(8, -1).astype(np.int64)


def pick8(x, idx, run):
    r = np.arange(len(x))
    return x[r[:, None], idx[r % (8 * run) // run]]


D, T, I, Q, X, E = 512, 1024, 512, 256, 32, 512


def setup_inputs():
    n = np.random.standard_normal
    idx = np.stack([np.random.permutation(T)[:I] for _ in range(8)])
    fd = mx_kscale(D)
    fi = mx_kscale(I)
    ti = np.ones((8, T))
    np.put_along_axis(ti, idx, np.tile(fi, (8, 1)), axis=1)
    return {
        "query": (n((D, Q)) * (np.arange(D)[:, None] // 64 == np.arange(Q) % 8) * 0.0625 * fd[:, None]).astype(np.float32),
        "keys": (n((D, T)) / fd[:, None]).astype(np.float32),
        "fa": (np.random.uniform(0.6, 1.0, (D, 1))).astype(np.float32),
        "fb": (np.random.uniform(-0.5, 0.5, (D, 1))).astype(np.float32),
        "size": (np.random.uniform(0.5, 2.0, (1, I)) * fi).astype(np.float32),
        "vals": (n((E, T)) / ti[np.arange(E) % 512 // 64]).astype(np.float32),
        "own": ((np.arange(E)[:, None] // 64 == np.arange(Q) % 8) * 1.0).astype(np.float32),
        "offs": striped8(idx),
    }


def reference(query, keys, fa, fb, size, vals, own, offs):
    idx = unstriped8(offs)
    k1 = np.pad(pick8(f64(keys), idx, 64), ((0, 0), (1, 0)))[:, :I]
    km = pick8(f64(keys), idx, 64) * f64(fa) + k1 * f64(fb)
    queryq = mxq(f64(query), 0, "e4m3")
    kmq = mxq(km, 0, "e4m3")
    a = queryq.T @ kmq
    p = np.exp(a - np.max(a, axis=1, keepdims=True))
    w = p * f64(size) / np.sum(p, axis=1, keepdims=True)
    wt = w.T
    vt = pick8(f64(vals), idx, 64).T
    vtq = mxq(vt, 0, "e4m3")
    wtq = mxq(wt, 0, "e4m3")
    o = vtq.T @ wtq
    ob = o * f64(own)
    y = ob.reshape(E, X, Q // X).sum(axis=2)
    return y

@@ -1,0 +1,198 @@
+from contextlib import ExitStack
+
+import concourse.mybir as mybir
+from concourse.masks import make_identity
+
+D, T, I, Q, X, E = 512, 1024, 512, 256, 32, 512
+P = 128
+PACK = 4
+HEADS = 8
+QT = Q // P
+FLOPS = 2 * Q * D * I + 2 * E * I * Q
+
+F32 = mybir.dt.float32
+BF16 = mybir.dt.bfloat16
+U32 = mybir.dt.uint32
+U16 = mybir.dt.uint16
+U8 = mybir.dt.uint8
+FP8X4 = mybir.dt.float8_e4m3fn_x4
+ACT = mybir.ActivationFunctionType
+ALU = mybir.AluOpType
+AXIS = mybir.AxisListType
+
+
+def tile_attend_ownlists_convkeys_kernel(tc, query, keys, fa, fb, size, vals, own, offs, out):
+    nc = tc.nc
+    with ExitStack() as ctx:
+        sb = ctx.enter_context(tc.tile_pool(name="sb", bufs=1))
+        ps = ctx.enter_context(tc.psum_pool(name="ps", bufs=1))
+
+        def tile(name, shape, dtype):
+            return sb.tile(shape, dtype, name=name, align_bytes=64)
+
+        def quantize(codes, scales, grouped):
+            nc.vector.quantize_mx(out=codes.bitcast(FP8X4), scales=scales, in_=grouped)
+
+        offsets = sb.tile([P, I // 16], U16, name="offsets")
+        key_rows = keys.rearrange("(p j) t -> p j t", j=PACK)
+        val_rows = vals.rearrange("(p j) t -> p j t", j=PACK)
+        key_pool = [tile(f"key_pool{j}", [P, T], F32) for j in range(PACK)]
+        val_pool = [tile(f"val_pool{j}", [P, T], F32) for j in range(PACK)]
+        q_raw = tile("q_raw", [P, PACK, Q], F32)
+        own_sb = tile("own_sb", [P, PACK, Q], F32)
+        fa_sb = tile("fa_sb", [P, PACK], F32)
+        fb_sb = tile("fb_sb", [P, PACK], F32)
+        size_sb = tile("size_sb", [P, PACK], F32)
+
+        nc.sync.dma_start(out=key_pool[0][:], in_=key_rows[:, 0, :])
+        nc.sync.dma_start(offsets[:], offs)
+        nc.scalar.dma_start(out=fa_sb[:], in_=fa.rearrange("(p j) o -> p (j o)", j=PACK))
+        nc.scalar.dma_start(out=fb_sb[:], in_=fb.rearrange("(p j) o -> p (j o)", j=PACK))
+        for j in range(1, PACK):
+            nc.sync.dma_start(out=key_pool[j][:], in_=key_rows[:, j, :])
+        nc.sync.dma_start(out=val_pool[0][:], in_=val_rows[:, 0, :])
+        nc.sync.dma_start(out=q_raw[:], in_=query.rearrange("(p j) q -> p j q", j=PACK))
+        nc.sync.dma_start(out=size_sb[:], in_=size.rearrange("o (s t) -> s (o t)", t=PACK))
+        for j in range(1, PACK):
+            nc.sync.dma_start(out=val_pool[j][:], in_=val_rows[:, j, :])
+        nc.sync.dma_start(out=own_sb[:], in_=own.rearrange("(p j) q -> p j q", j=PACK))
+
+        warm = tile("warm", [P, 1], F32)
+        ident = tile("ident", [P, P], F32)
+        make_identity(nc, ident[:])
+        nc.scalar.activation(out=warm[:], in_=ident[:, 0:1], func=ACT.Exp)
+
+        here = tile("here", [P, PACK, I], F32)
+        before = tile("before", [P, PACK, I], F32)
+        nc.gpsimd.memset(before[:, :, 0:1], 0.0)
+        for j in range(PACK):
+            picked = tile(f"picked{j}", [P, I], F32)
+            nc.vector.tensor_copy(picked[:], key_pool[j][:].indirect(offsets[:]))
+            nc.scalar.activation(out=before[:, j, 1:I], in_=picked[:, 0 : I - 1], func=ACT.Copy, scale=fb_sb[:, j : j + 1])
+            nc.scalar.activation(out=here[:, j, :], in_=picked[:], func=ACT.Copy, scale=fa_sb[:, j : j + 1])
+
+        v_codes = tile("v_codes", [P, E], U32)
+        v_scales = tile("v_scales", [P, E], U8)
+        v_grouped = tile("v_grouped", [P, PACK, P, PACK], BF16)
+        v_banks = [ps.tile([P, 2, 2, P], F32, name=f"v_bank{b}") for b in range(2)]
+
+        def gather_vals(j):
+            v_picked = tile(f"v_picked{j}", [P, I], BF16)
+            nc.vector.tensor_copy(v_picked[:], val_pool[j][:].indirect(offsets[:]))
+            words = v_picked[:].bitcast(F32)
+            for u in range(2):
+                nc.tensor.transpose(v_banks[j // 2][:, j % 2, u, :], words[:, u : I // 2 : 2], ident[:])
+            nc.scalar.copy(
+                out=v_grouped[:, j].rearrange("s e t -> s (e t)").bitcast(F32).rearrange("s (e u) -> s e u", u=2),
+                in_=v_banks[j // 2][:, j % 2].rearrange("s u e -> s e u"),
+            )
+
+        def quantize_vals(b):
+            cols = slice(b * 2 * P, (b + 1) * 2 * P)
+            quantize(v_codes[:, cols], v_scales[:, cols], v_grouped[:, 2 * b : 2 * b + 2].rearrange("s j e t -> s (j e t)"))
+
+        gather_vals(0)
+
+        q_grouped = tile("q_grouped", [P, Q, PACK], BF16)
+        nc.scalar.copy(
+            out=q_grouped[:].rearrange("p (c i) j -> p c j i", i=4),
+            in_=q_raw[:].rearrange("p j (c i) -> p c j i", i=4),
+        )
+
+        km = tile("km", [P, I, PACK], BF16)
+        k_codes = tile("k_codes", [P, I], U32)
+        k_scales = tile("k_scales", [P, I], U8)
+        halves = [slice(0, I)]
+        for cols in halves:
+            nc.vector.tensor_tensor(
+                km[:, cols, :].rearrange("p (c i) j -> p c j i", i=4),
+                here[:, :, cols].rearrange("p j (c i) -> p c j i", i=4),
+                before[:, :, cols].rearrange("p j (c i) -> p c j i", i=4),
+                ALU.add,
+            )
+        q_codes = tile("q_codes", [P, Q], U32)
+        q_scales = tile("q_scales", [P, Q], U8)
+        quantize(q_codes[:], q_scales[:], q_grouped[:].rearrange("p q j -> p (q j)"))
+        for cols in halves:
+            quantize(k_codes[:, cols], k_scales[:, cols], km[:, cols, :].rearrange("p i j -> p (i j)"))
+
+        size_bank = ps.tile([P, PACK, P], F32, name="size_bank")
+        for t in range(PACK):
+            nc.tensor.transpose(size_bank[:, t, :], size_sb[:, t : t + 1].to_broadcast([P, P]), ident[:])
+
+        banks = [ps.tile([P, I], F32, name=f"score_bank{h}") for h in range(QT)]
+        for h in range(QT):
+            cols = slice(h * P, (h + 1) * P)
+            nc.tensor.matmul_mx(
+                out=banks[h][:], lhsT=q_codes[:, cols].bitcast(FP8X4), lhsT_scale=q_scales[:, cols],
+                rhs=k_codes[:].bitcast(FP8X4), rhs_scale=k_scales[:], start=True, stop=True,
+            )
+        gather_vals(1)
+        probs, inv = [], []
+        for h in range(QT):
+            neg_max = tile(f"neg_max{h}", [P, 1], F32)
+            nc.vector.tensor_reduce(neg_max[:], banks[h][:], AXIS.X, ALU.max, negate=True)
+            prob = tile(f"prob{h}", [P, I], F32)
+            total = tile(f"total{h}", [P, 1], F32)
+            nc.scalar.activation(out=prob[:], in_=banks[h][:], func=ACT.Exp, bias=neg_max[:], accum_out=total[:])
+            probs.append(prob)
+            inv.append(total)
+        gather_vals(2)
+        quantize_vals(0)
+        w_grouped = []
+        for h in range(QT):
+            recip = tile(f"recip{h}", [P, 1], F32)
+            nc.vector.reciprocal(recip[:], inv[h][:])
+            w = tile(f"w{h}", [P, I], BF16)
+            nc.vector.scalar_tensor_tensor(
+                w[:].rearrange("q (s t) -> q s t", t=PACK),
+                probs[h][:].rearrange("q (s t) -> q s t", t=PACK),
+                recip[:],
+                size_bank[:].rearrange("q t s -> q s t"),
+                ALU.mult,
+                ALU.mult,
+            )
+            words = w[:].bitcast(F32)
+            w_bank = ps.tile([P, 2, P], F32, name=f"w_bank{h}")
+            for u in range(2):
+                nc.tensor.transpose(w_bank[:, u, :], words[:, u : I // 2 : 2], ident[:])
+            grouped = tile(f"w_grouped{h}", [P, P * PACK], BF16)
+            nc.scalar.copy(
+                out=grouped[:].bitcast(F32).rearrange("s (q u) -> s q u", u=2),
+                in_=w_bank[:].rearrange("s u q -> s q u"),
+            )
+            w_grouped.append(grouped)
+        gather_vals(3)
+        w_ops = []
+        for h in range(QT):
+            w_codes = tile(f"w_codes{h}", [P, P], U32)
+            w_scales = tile(f"w_scales{h}", [P, P], U8)
+            quantize(w_codes[:], w_scales[:], w_grouped[h][:])
+            w_ops.append((w_codes, w_scales))
+        quantize_vals(1)
+
+        y = tile("y", [P, PACK, X], F32)
+        places = P // HEADS
+        for h in range(QT):
+            o_bank = banks[h][:].rearrange("p (j q) -> p j q", j=PACK)
+            w_codes, w_scales = w_ops[h]
+            for j in range(PACK):
+                cols = slice(j * P, (j + 1) * P)
+                nc.tensor.matmul_mx(
+                    out=o_bank[:, j, :], lhsT=v_codes[:, cols].bitcast(FP8X4), lhsT_scale=v_scales[:, cols],
+                    rhs=w_codes[:].bitcast(FP8X4), rhs_scale=w_scales[:], start=True, stop=True,
+                )
+        masked = []
+        for h in range(QT):
+            o_bank = banks[h][:].rearrange("p (j q) -> p j q", j=PACK)
+            ob = tile(f"ob{h}", [P, PACK, P], F32)
+            nc.vector.tensor_tensor(ob[:], o_bank, own_sb[:, :, h * P : (h + 1) * P], ALU.mult)
+            masked.append(ob)
+        for h in range(QT):
+            nc.vector.tensor_reduce(
+                y[:, :, h * places : (h + 1) * places],
+                masked[h][:].rearrange("p j (x g) -> p j x g", g=HEADS),
+                AXIS.X,
+                ALU.add,
+            )
+        nc.sync.dma_start(out=out.rearrange("(p j) x -> p j x", j=PACK), in_=y[:])

@@ -27,8 +27,8 @@ def tile_attend_ownlists_convkeys_kernel(tc, query, keys, fa, fb, size, vals, ow
         sb = ctx.enter_context(tc.tile_pool(name="sb", bufs=1))
         ps = ctx.enter_context(tc.psum_pool(name="ps", bufs=1))
 
-        def tile(name, shape, dtype):
-            return sb.tile(shape, dtype, name=name, align_bytes=64)
+        def tile(name, shape, dtype, tag=""):
+            return sb.tile(shape, dtype, name=name, tag=tag or name, align_bytes=64)
 
         def quantize(codes, scales, grouped):
             nc.vector.quantize_mx(out=codes.bitcast(FP8X4), scales=scales, in_=grouped)
@@ -50,10 +50,9 @@ def tile_attend_ownlists_convkeys_kernel(tc, query, keys, fa, fb, size, vals, ow
         nc.scalar.dma_start(out=fb_sb[:], in_=fb.rearrange("(p j) o -> p (j o)", j=PACK))
         for j in range(1, PACK):
             nc.sync.dma_start(out=key_pool[j][:], in_=key_rows[:, j, :])
-        nc.sync.dma_start(out=val_pool[0][:], in_=val_rows[:, 0, :])
         nc.sync.dma_start(out=q_raw[:], in_=query.rearrange("(p j) q -> p j q", j=PACK))
         nc.sync.dma_start(out=size_sb[:], in_=size.rearrange("o (s t) -> s (o t)", t=PACK))
-        for j in range(1, PACK):
+        for j in range(PACK):
             nc.sync.dma_start(out=val_pool[j][:], in_=val_rows[:, j, :])
         nc.sync.dma_start(out=own_sb[:], in_=own.rearrange("(p j) q -> p j q", j=PACK))
 
@@ -64,34 +63,42 @@ def tile_attend_ownlists_convkeys_kernel(tc, query, keys, fa, fb, size, vals, ow
 
         here = tile("here", [P, PACK, I], F32)
         before = tile("before", [P, PACK, I], F32)
-        nc.gpsimd.memset(before[:, :, 0:1], 0.0)
+        nc.vector.memset(before[:, :, 0:1], 0.0)
         for j in range(PACK):
             picked = tile(f"picked{j}", [P, I], F32)
             nc.vector.tensor_copy(picked[:], key_pool[j][:].indirect(offsets[:]))
             nc.scalar.activation(out=before[:, j, 1:I], in_=picked[:, 0 : I - 1], func=ACT.Copy, scale=fb_sb[:, j : j + 1])
-            nc.scalar.activation(out=here[:, j, :], in_=picked[:], func=ACT.Copy, scale=fa_sb[:, j : j + 1])
+            if j < PACK - 1:
+                nc.scalar.activation(out=here[:, j, :], in_=picked[:], func=ACT.Copy, scale=fa_sb[:, j : j + 1])
+            else:
+                nc.vector.tensor_scalar_mul(here[:, j, :], picked[:], fa_sb[:, j : j + 1])
 
-        v_codes = tile("v_codes", [P, E], U32)
-        v_scales = tile("v_scales", [P, E], U8)
-        v_grouped = tile("v_grouped", [P, PACK, P, PACK], BF16)
-        v_banks = [ps.tile([P, 2, 2, P], F32, name=f"v_bank{b}") for b in range(2)]
+        v_scales = [tile(f"v_scales{b}", [P, 2 * P], U8) for b in range(2)]
+        banks = [ps.tile([P, I], F32, name=f"score_bank{h}") for h in range(QT)]
+        v_banks = [ps.tile([P, 2, 2, P], F32, name=f"v_bank{b}")[:] for b in range(2)]
 
-        def gather_vals(j):
-            v_picked = tile(f"v_picked{j}", [P, I], BF16)
-            nc.vector.tensor_copy(v_picked[:], val_pool[j][:].indirect(offsets[:]))
+        def gather_vals(j, tag=""):
+            v_picked = tile(f"v_picked{j}", [P, I], BF16, tag=tag)
+            if j in (1, 2):
+                rounded = tile(f"v_rounded{j}", [P, T], BF16)
+                nc.scalar.activation(out=rounded[:], in_=val_pool[j][:], func=ACT.Copy)
+                nc.scalar.activation(out=v_picked[:], in_=rounded[:].indirect(offsets[:]), func=ACT.Copy)
+            else:
+                nc.vector.tensor_copy(v_picked[:], val_pool[j][:].indirect(offsets[:]))
+            return v_picked
+
+        def turn_vals(j, v_picked):
             words = v_picked[:].bitcast(F32)
             for u in range(2):
                 nc.tensor.transpose(v_banks[j // 2][:, j % 2, u, :], words[:, u : I // 2 : 2], ident[:])
+
+        def ungroup_vals(b, tag):
+            v_grouped = tile(f"v_grouped{b}", [P, 2 * P * PACK], BF16, tag=tag)
             nc.scalar.copy(
-                out=v_grouped[:, j].rearrange("s e t -> s (e t)").bitcast(F32).rearrange("s (e u) -> s e u", u=2),
-                in_=v_banks[j // 2][:, j % 2].rearrange("s u e -> s e u"),
+                out=v_grouped[:].bitcast(F32).rearrange("s (j e u) -> s j e u", j=2, u=2),
+                in_=v_banks[b].rearrange("s j u e -> s j e u"),
             )
-
-        def quantize_vals(b):
-            cols = slice(b * 2 * P, (b + 1) * 2 * P)
-            quantize(v_codes[:, cols], v_scales[:, cols], v_grouped[:, 2 * b : 2 * b + 2].rearrange("s j e t -> s (j e t)"))
-
-        gather_vals(0)
+            return v_grouped
 
         q_grouped = tile("q_grouped", [P, Q, PACK], BF16)
         nc.scalar.copy(
@@ -99,6 +106,7 @@ def tile_attend_ownlists_convkeys_kernel(tc, query, keys, fa, fb, size, vals, ow
             in_=q_raw[:].rearrange("p j (c i) -> p c j i", i=4),
         )
 
+        early = [gather_vals(j) for j in (1, 2)]
         km = tile("km", [P, I, PACK], BF16)
         k_codes = tile("k_codes", [P, I], U32)
         k_scales = tile("k_scales", [P, I], U8)
@@ -116,79 +124,86 @@ def tile_attend_ownlists_convkeys_kernel(tc, query, keys, fa, fb, size, vals, ow
         for cols in halves:
             quantize(k_codes[:, cols], k_scales[:, cols], km[:, cols, :].rearrange("p i j -> p (i j)"))
 
-        size_bank = ps.tile([P, PACK, P], F32, name="size_bank")
+        size_bank = ps.tile([P, 2, 2, P], F32, name="size_bank")
         for t in range(PACK):
-            nc.tensor.transpose(size_bank[:, t, :], size_sb[:, t : t + 1].to_broadcast([P, P]), ident[:])
+            nc.tensor.transpose(size_bank[:, t % 2, t // 2, :], size_sb[:, t : t + 1].to_broadcast([P, P]), ident[:])
 
-        banks = [ps.tile([P, I], F32, name=f"score_bank{h}") for h in range(QT)]
         for h in range(QT):
             cols = slice(h * P, (h + 1) * P)
             nc.tensor.matmul_mx(
                 out=banks[h][:], lhsT=q_codes[:, cols].bitcast(FP8X4), lhsT_scale=q_scales[:, cols],
                 rhs=k_codes[:].bitcast(FP8X4), rhs_scale=k_scales[:], start=True, stop=True,
             )
-        gather_vals(1)
+        turn_vals(1, early[0])
+        turn_vals(0, gather_vals(0))
+        turn_vals(2, early[1])
         probs, inv = [], []
         for h in range(QT):
             neg_max = tile(f"neg_max{h}", [P, 1], F32)
             nc.vector.tensor_reduce(neg_max[:], banks[h][:], AXIS.X, ALU.max, negate=True)
-            prob = tile(f"prob{h}", [P, I], F32)
+            prob = tile(f"prob{h}", [P, I], F32, tag="v_rounded2" if h == 0 else "")
             total = tile(f"total{h}", [P, 1], F32)
-            nc.scalar.activation(out=prob[:], in_=banks[h][:], func=ACT.Exp, bias=neg_max[:], accum_out=total[:])
+            nc.scalar.activation(
+                out=prob[:].rearrange("q (u s e) -> q u s e", u=2, e=2),
+                in_=banks[h][:].rearrange("q (s u e) -> q u s e", u=2, e=2),
+                func=ACT.Exp, bias=neg_max[:], accum_out=total[:],
+            )
             probs.append(prob)
             inv.append(total)
-        gather_vals(2)
-        quantize_vals(0)
+        turn_vals(3, gather_vals(3, tag="q_codes"))
+        v_grouped = [ungroup_vals(0, f"neg_max{QT - 1}")]
         w_grouped = []
         for h in range(QT):
             recip = tile(f"recip{h}", [P, 1], F32)
             nc.vector.reciprocal(recip[:], inv[h][:])
             w = tile(f"w{h}", [P, I], BF16)
             nc.vector.scalar_tensor_tensor(
-                w[:].rearrange("q (s t) -> q s t", t=PACK),
-                probs[h][:].rearrange("q (s t) -> q s t", t=PACK),
+                w[:].rearrange("q (n e) -> q n e", e=2),
+                probs[h][:].rearrange("q (n e) -> q n e", e=2),
                 recip[:],
-                size_bank[:].rearrange("q t s -> q s t"),
+                size_bank[:].rearrange("q e u s -> q (u s) e"),
                 ALU.mult,
                 ALU.mult,
             )
+            if h == 0:
+                v_grouped.append(ungroup_vals(1, "v_rounded2"))
             words = w[:].bitcast(F32)
             w_bank = ps.tile([P, 2, P], F32, name=f"w_bank{h}")
             for u in range(2):
-                nc.tensor.transpose(w_bank[:, u, :], words[:, u : I // 2 : 2], ident[:])
+                nc.tensor.transpose(w_bank[:, u, :], words[:, u * P : (u + 1) * P], ident[:])
             grouped = tile(f"w_grouped{h}", [P, P * PACK], BF16)
             nc.scalar.copy(
                 out=grouped[:].bitcast(F32).rearrange("s (q u) -> s q u", u=2),
                 in_=w_bank[:].rearrange("s u q -> s q u"),
             )
             w_grouped.append(grouped)
-        gather_vals(3)
+        v_codes = [tile("v_codes0", [P, 2 * P], U32, tag=f"prob{QT - 1}"), tile("v_codes1", [P, 2 * P], U32)]
         w_ops = []
         for h in range(QT):
+            quantize(v_codes[h][:], v_scales[h][:], v_grouped[h][:])
             w_codes = tile(f"w_codes{h}", [P, P], U32)
             w_scales = tile(f"w_scales{h}", [P, P], U8)
             quantize(w_codes[:], w_scales[:], w_grouped[h][:])
             w_ops.append((w_codes, w_scales))
-        quantize_vals(1)
 
         y = tile("y", [P, PACK, X], F32)
         places = P // HEADS
+        o_banks = [b[:].rearrange("p (j q) -> p j q", j=PACK) for b in banks]
         for h in range(QT):
-            o_bank = banks[h][:].rearrange("p (j q) -> p j q", j=PACK)
+            o_bank = o_banks[h]
             w_codes, w_scales = w_ops[h]
             for j in range(PACK):
-                cols = slice(j * P, (j + 1) * P)
+                cols = slice(j % 2 * P, (j % 2 + 1) * P)
                 nc.tensor.matmul_mx(
-                    out=o_bank[:, j, :], lhsT=v_codes[:, cols].bitcast(FP8X4), lhsT_scale=v_scales[:, cols],
+                    out=o_bank[:, j, :], lhsT=v_codes[j // 2][:, cols].bitcast(FP8X4), lhsT_scale=v_scales[j // 2][:, cols],
                     rhs=w_codes[:].bitcast(FP8X4), rhs_scale=w_scales[:], start=True, stop=True,
                 )
         masked = []
         for h in range(QT):
-            o_bank = banks[h][:].rearrange("p (j q) -> p j q", j=PACK)
+            o_bank = o_banks[h]
             ob = tile(f"ob{h}", [P, PACK, P], F32)
             nc.vector.tensor_tensor(ob[:], o_bank, own_sb[:, :, h * P : (h + 1) * P], ALU.mult)
             masked.append(ob)
-        for h in range(QT):
             nc.vector.tensor_reduce(
                 y[:, :, h * places : (h + 1) * places],
                 masked[h][:].rearrange("p j (x g) -> p j x g", g=HEADS),

from contextlib import ExitStack

import concourse.mybir as mybir
from concourse.masks import make_identity

D, T, I, Q, X, E = 512, 1024, 512, 256, 32, 512
P = 128
PACK = 4
HEADS = 8
QT = Q // P
FLOPS = 2 * Q * D * I + 2 * E * I * Q

F32 = mybir.dt.float32
BF16 = mybir.dt.bfloat16
U32 = mybir.dt.uint32
U16 = mybir.dt.uint16
U8 = mybir.dt.uint8
FP8X4 = mybir.dt.float8_e4m3fn_x4
ACT = mybir.ActivationFunctionType
ALU = mybir.AluOpType
AXIS = mybir.AxisListType


def tile_attend_ownlists_convkeys_kernel(tc, query, keys, fa, fb, size, vals, own, offs, out):
    nc = tc.nc
    with ExitStack() as ctx:
        sb = ctx.enter_context(tc.tile_pool(name="sb", bufs=1))
        ps = ctx.enter_context(tc.psum_pool(name="ps", bufs=1))

        def tile(name, shape, dtype, tag=""):
            return sb.tile(shape, dtype, name=name, tag=tag or name, align_bytes=64)

        def quantize(codes, scales, grouped):
            nc.vector.quantize_mx(out=codes.bitcast(FP8X4), scales=scales, in_=grouped)

        offsets = sb.tile([P, I // 16], U16, name="offsets")
        key_rows = keys.rearrange("(p j) t -> p j t", j=PACK)
        val_rows = vals.rearrange("(p j) t -> p j t", j=PACK)
        key_pool = [tile(f"key_pool{j}", [P, T], F32) for j in range(PACK)]
        val_pool = [tile(f"val_pool{j}", [P, T], F32) for j in range(PACK)]
        q_raw = tile("q_raw", [P, PACK, Q], F32)
        own_sb = tile("own_sb", [P, PACK, Q], F32)
        fa_sb = tile("fa_sb", [P, PACK], F32)
        fb_sb = tile("fb_sb", [P, PACK], F32)
        size_sb = tile("size_sb", [P, PACK], F32)

        nc.sync.dma_start(out=key_pool[0][:], in_=key_rows[:, 0, :])
        nc.sync.dma_start(offsets[:], offs)
        nc.scalar.dma_start(out=fa_sb[:], in_=fa.rearrange("(p j) o -> p (j o)", j=PACK))
        nc.scalar.dma_start(out=fb_sb[:], in_=fb.rearrange("(p j) o -> p (j o)", j=PACK))
        for j in range(1, PACK):
            nc.sync.dma_start(out=key_pool[j][:], in_=key_rows[:, j, :])
        nc.sync.dma_start(out=q_raw[:], in_=query.rearrange("(p j) q -> p j q", j=PACK))
        nc.sync.dma_start(out=size_sb[:], in_=size.rearrange("o (s t) -> s (o t)", t=PACK))
        for j in range(PACK):
            nc.sync.dma_start(out=val_pool[j][:], in_=val_rows[:, j, :])
        nc.sync.dma_start(out=own_sb[:], in_=own.rearrange("(p j) q -> p j q", j=PACK))

        warm = tile("warm", [P, 1], F32)
        ident = tile("ident", [P, P], F32)
        make_identity(nc, ident[:])
        nc.scalar.activation(out=warm[:], in_=ident[:, 0:1], func=ACT.Exp)

        here = tile("here", [P, PACK, I], F32)
        before = tile("before", [P, PACK, I], F32)
        nc.vector.memset(before[:, :, 0:1], 0.0)
        for j in range(PACK):
            picked = tile(f"picked{j}", [P, I], F32)
            nc.vector.tensor_copy(picked[:], key_pool[j][:].indirect(offsets[:]))
            nc.scalar.activation(out=before[:, j, 1:I], in_=picked[:, 0 : I - 1], func=ACT.Copy, scale=fb_sb[:, j : j + 1])
            if j < PACK - 1:
                nc.scalar.activation(out=here[:, j, :], in_=picked[:], func=ACT.Copy, scale=fa_sb[:, j : j + 1])
            else:
                nc.vector.tensor_scalar_mul(here[:, j, :], picked[:], fa_sb[:, j : j + 1])

        v_scales = [tile(f"v_scales{b}", [P, 2 * P], U8) for b in range(2)]
        banks = [ps.tile([P, I], F32, name=f"score_bank{h}") for h in range(QT)]
        v_banks = [ps.tile([P, 2, 2, P], F32, name=f"v_bank{b}")[:] for b in range(2)]

        def gather_vals(j, tag=""):
            v_picked = tile(f"v_picked{j}", [P, I], BF16, tag=tag)
            if j in (1, 2):
                rounded = tile(f"v_rounded{j}", [P, T], BF16)
                nc.scalar.activation(out=rounded[:], in_=val_pool[j][:], func=ACT.Copy)
                nc.scalar.activation(out=v_picked[:], in_=rounded[:].indirect(offsets[:]), func=ACT.Copy)
            else:
                nc.vector.tensor_copy(v_picked[:], val_pool[j][:].indirect(offsets[:]))
            return v_picked

        def turn_vals(j, v_picked):
            words = v_picked[:].bitcast(F32)
            for u in range(2):
                nc.tensor.transpose(v_banks[j // 2][:, j % 2, u, :], words[:, u : I // 2 : 2], ident[:])

        def ungroup_vals(b, tag):
            v_grouped = tile(f"v_grouped{b}", [P, 2 * P * PACK], BF16, tag=tag)
            nc.scalar.copy(
                out=v_grouped[:].bitcast(F32).rearrange("s (j e u) -> s j e u", j=2, u=2),
                in_=v_banks[b].rearrange("s j u e -> s j e u"),
            )
            return v_grouped

        q_grouped = tile("q_grouped", [P, Q, PACK], BF16)
        nc.scalar.copy(
            out=q_grouped[:].rearrange("p (c i) j -> p c j i", i=4),
            in_=q_raw[:].rearrange("p j (c i) -> p c j i", i=4),
        )

        early = [gather_vals(j) for j in (1, 2)]
        km = tile("km", [P, I, PACK], BF16)
        k_codes = tile("k_codes", [P, I], U32)
        k_scales = tile("k_scales", [P, I], U8)
        halves = [slice(0, I)]
        for cols in halves:
            nc.vector.tensor_tensor(
                km[:, cols, :].rearrange("p (c i) j -> p c j i", i=4),
                here[:, :, cols].rearrange("p j (c i) -> p c j i", i=4),
                before[:, :, cols].rearrange("p j (c i) -> p c j i", i=4),
                ALU.add,
            )
        q_codes = tile("q_codes", [P, Q], U32)
        q_scales = tile("q_scales", [P, Q], U8)
        quantize(q_codes[:], q_scales[:], q_grouped[:].rearrange("p q j -> p (q j)"))
        for cols in halves:
            quantize(k_codes[:, cols], k_scales[:, cols], km[:, cols, :].rearrange("p i j -> p (i j)"))

        size_bank = ps.tile([P, 2, 2, P], F32, name="size_bank")
        for t in range(PACK):
            nc.tensor.transpose(size_bank[:, t % 2, t // 2, :], size_sb[:, t : t + 1].to_broadcast([P, P]), ident[:])

        for h in range(QT):
            cols = slice(h * P, (h + 1) * P)
            nc.tensor.matmul_mx(
                out=banks[h][:], lhsT=q_codes[:, cols].bitcast(FP8X4), lhsT_scale=q_scales[:, cols],
                rhs=k_codes[:].bitcast(FP8X4), rhs_scale=k_scales[:], start=True, stop=True,
            )
        turn_vals(1, early[0])
        turn_vals(0, gather_vals(0))
        turn_vals(2, early[1])
        probs, inv = [], []
        for h in range(QT):
            neg_max = tile(f"neg_max{h}", [P, 1], F32)
            nc.vector.tensor_reduce(neg_max[:], banks[h][:], AXIS.X, ALU.max, negate=True)
            prob = tile(f"prob{h}", [P, I], F32, tag="v_rounded2" if h == 0 else "")
            total = tile(f"total{h}", [P, 1], F32)
            nc.scalar.activation(
                out=prob[:].rearrange("q (u s e) -> q u s e", u=2, e=2),
                in_=banks[h][:].rearrange("q (s u e) -> q u s e", u=2, e=2),
                func=ACT.Exp, bias=neg_max[:], accum_out=total[:],
            )
            probs.append(prob)
            inv.append(total)
        turn_vals(3, gather_vals(3, tag="q_codes"))
        v_grouped = [ungroup_vals(0, f"neg_max{QT - 1}")]
        w_grouped = []
        for h in range(QT):
            recip = tile(f"recip{h}", [P, 1], F32)
            nc.vector.reciprocal(recip[:], inv[h][:])
            w = tile(f"w{h}", [P, I], BF16)
            nc.vector.scalar_tensor_tensor(
                w[:].rearrange("q (n e) -> q n e", e=2),
                probs[h][:].rearrange("q (n e) -> q n e", e=2),
                recip[:],
                size_bank[:].rearrange("q e u s -> q (u s) e"),
                ALU.mult,
                ALU.mult,
            )
            if h == 0:
                v_grouped.append(ungroup_vals(1, "v_rounded2"))
            words = w[:].bitcast(F32)
            w_bank = ps.tile([P, 2, P], F32, name=f"w_bank{h}")
            for u in range(2):
                nc.tensor.transpose(w_bank[:, u, :], words[:, u * P : (u + 1) * P], ident[:])
            grouped = tile(f"w_grouped{h}", [P, P * PACK], BF16)
            nc.scalar.copy(
                out=grouped[:].bitcast(F32).rearrange("s (q u) -> s q u", u=2),
                in_=w_bank[:].rearrange("s u q -> s q u"),
            )
            w_grouped.append(grouped)
        v_codes = [tile("v_codes0", [P, 2 * P], U32, tag=f"prob{QT - 1}"), tile("v_codes1", [P, 2 * P], U32)]
        w_ops = []
        for h in range(QT):
            quantize(v_codes[h][:], v_scales[h][:], v_grouped[h][:])
            w_codes = tile(f"w_codes{h}", [P, P], U32)
            w_scales = tile(f"w_scales{h}", [P, P], U8)
            quantize(w_codes[:], w_scales[:], w_grouped[h][:])
            w_ops.append((w_codes, w_scales))

        y = tile("y", [P, PACK, X], F32)
        places = P // HEADS
        o_banks = [b[:].rearrange("p (j q) -> p j q", j=PACK) for b in banks]
        for h in range(QT):
            o_bank = o_banks[h]
            w_codes, w_scales = w_ops[h]
            for j in range(PACK):
                cols = slice(j % 2 * P, (j % 2 + 1) * P)
                nc.tensor.matmul_mx(
                    out=o_bank[:, j, :], lhsT=v_codes[j // 2][:, cols].bitcast(FP8X4), lhsT_scale=v_scales[j // 2][:, cols],
                    rhs=w_codes[:].bitcast(FP8X4), rhs_scale=w_scales[:], start=True, stop=True,
                )
        masked = []
        for h in range(QT):
            o_bank = o_banks[h]
            ob = tile(f"ob{h}", [P, PACK, P], F32)
            nc.vector.tensor_tensor(ob[:], o_bank, own_sb[:, :, h * P : (h + 1) * P], ALU.mult)
            masked.append(ob)
            nc.vector.tensor_reduce(
                y[:, :, h * places : (h + 1) * places],
                masked[h][:].rearrange("p j (x g) -> p j x g", g=HEADS),
                AXIS.X,
                ALU.add,
            )
        nc.sync.dma_start(out=out.rearrange("(p j) x -> p j x", j=PACK), in_=y[:])
